import numpy as np
import ml_dtypes


def mxq(x, axis, fmt="e4m3"):
    dtype, down = {"e4m3": (ml_dtypes.float8_e4m3fn, 7), "e5m2": (ml_dtypes.float8_e5m2, 14)}[fmt]
    v = np.moveaxis(np.asarray(x, np.float32).astype(ml_dtypes.bfloat16).astype(np.float64), axis, -1)
    blocks = v.reshape(v.shape[:-1] + (-1, 32))
    amax = np.abs(blocks).max(-1, keepdims=True)
    byte = np.maximum(np.where(amax > 0, np.frexp(amax)[1] - 1 + 127, 0) - down, 1)
    scale = np.exp2(byte - 127.0)
    codes = (blocks / scale).astype(np.float32).astype(dtype).astype(np.float64)
    return np.moveaxis((codes * scale).reshape(v.shape), -1, axis)


WIDE = False


def mx_kscale(k):
    if not WIDE:
        return np.ones(k)
    levels = np.array([10, -10, 5, -5, 0])
    if k % 512:
        return np.exp2(np.random.permutation(np.resize(levels, k // 32))).repeat(32)
    a = np.empty((k // 512, 16))
    for p in range(k // 512):
        a[p, :8] = np.random.permutation(np.resize(levels, 8))
        for g in range(8):
            far = levels[np.abs(levels - a[p, g]) >= 10]
            a[p, g + 8] = far[np.random.randint(len(far))]
    return np.exp2(a.ravel()).repeat(32)


BF16 = ml_dtypes.bfloat16


def bf(x):
    return np.asarray(x, np.float32).astype(BF16)


def f64(x):
    return np.asarray(x).astype(np.float64)


E2M1 = np.array([0.0, 0.5, 1.0, 1.5, 2.0, 3.0, 4.0, 6.0, -0.0, -0.5, -1.0, -1.5, -2.0, -3.0, -4.0, -6.0])


def pack_weight(w, fmt):
    k, n = w.shape
    w = f64(bf(w)).reshape(k // 32, 32, n)
    amax = np.abs(w).max(1)
    if fmt == "e4m3":
        byte = np.frexp(amax)[1] - 1 + 127 - 7
    else:
        mant, ex = np.frexp(amax / 6.0)
        byte = np.where(mant > 0.5, ex, ex - 1) + 127
    byte = np.clip(np.where(amax > 0, byte, 1), 1, 254)
    scaled = (w * np.exp2(127.0 - byte)[:, None, :]).reshape(k, n).astype(np.float32)
    by_word = np.ascontiguousarray(scaled.reshape(k // 512, 128, 4, n).transpose(0, 1, 3, 2))
    if fmt == "e4m3":
        words = by_word.astype(ml_dtypes.float8_e4m3fn).view(np.uint8)
    else:
        c = by_word.astype(ml_dtypes.float4_e2m1fn).view(np.uint8) & 0xF
        words = c[..., 0::2] | (c[..., 1::2] << 4)
    return np.ascontiguousarray(words), np.ascontiguousarray(byte.astype(np.uint8).reshape(k // 512, 16, n))


def unpack_weight(words, scales, fmt):
    g, p, n, _ = words.shape
    if fmt == "e4m3":
        vals = np.ascontiguousarray(words).view(ml_dtypes.float8_e4m3fn).astype(np.float64)
    else:
        nib = np.empty((g, p, n, 4), np.uint8)
        nib[..., 0::2] = words & 0xF
        nib[..., 1::2] = words >> 4
        vals = E2M1[nib]
    vals = vals * np.repeat(np.exp2(scales.astype(np.float64) - 127.0), 8, axis=1)[..., None]
    return vals.transpose(0, 1, 3, 2).reshape(g * 512, n)
def pack4(w):
    words, scales = pack_weight(w, "e2m1")
    return words.reshape(words.shape[0], 128, -1), scales


def unpack4(words, scales):
    return unpack_weight(words.reshape(words.shape[0], 128, -1, 2), scales, "e2m1")


def planes(Y):
    n, m = Y.shape
    b = f64(bf(Y)).reshape(n // 32, 32, m)
    amax = np.abs(b).max(1)
    byte = np.clip(np.where(amax > 0, np.frexp(amax)[1] - 1 + 127 - 7, 1), 1, 254)
    codes = (b * np.exp2(127.0 - byte)[:, None, :]).reshape(n, m).astype(np.float32).astype(ml_dtypes.float8_e4m3fn).view(np.uint8)
    words = codes.reshape(n // 512, 128, 4, m).transpose(0, 1, 3, 2)
    return np.ascontiguousarray(words), np.ascontiguousarray(byte.astype(np.uint8).reshape(n // 512, 16, m))


M, K, F = 1024, 2048, 1536

def setup_inputs():
    s = mx_kscale(K)
    t = mx_kscale(F)
    x = np.random.randn(K, M)
    x = x - x.mean(axis=1, keepdims=True)
    x_words, x_scales = pack_weight(x * s[:, None], "e4m3")
    h = np.random.randn(K, F) / np.sqrt(K)
    h_words, h_scales = pack4(h / s[:, None] * t[None, :])
    d = np.random.randn(M, F) * np.exp(0.8 * np.random.randn(M, 1)) / np.sqrt(F)
    d = d - d.mean(axis=0, keepdims=True)
    return {
        "x_words": x_words,
        "x_scales": x_scales,
        "h_words": h_words,
        "h_scales": h_scales,
        "r_inv": bf(np.exp(0.4 * np.random.randn(F))),
        "d": bf(d / t[None, :]),
        "shift": bf(8.0 * (1.0 + 0.1 * np.random.randn(M))),
    }

def reference(x_words, x_scales, h_words, h_scales, r_inv, d, shift):
    xt = unpack_weight(x_words, x_scales, "e4m3")
    h = unpack4(h_words, h_scales)
    z = (xt.T @ h) * f64(r_inv)
    p = mxq(z, 1, "e4m3") @ mxq(f64(d), 1, "e4m3").T
    y = p + f64(shift) * np.eye(M)
    words, scales = planes(y.T)
    return y, words, scales

from contextlib import ExitStack

import concourse.mybir as mybir
from concourse.masks import make_identity

M, K, F = 1024, 2048, 1536
FLOPS = 2 * M * K * F + 2 * M * M * F

F32 = mybir.dt.float32
BF16 = mybir.dt.bfloat16
I32 = mybir.dt.int32
U8 = mybir.dt.uint8
FP8X4 = mybir.dt.float8_e4m3fn_x4
FP4X4 = mybir.dt.float4_e2m1fn_x4
COPY = mybir.ActivationFunctionType.Copy
ALU = mybir.AluOpType

P = 128
N = 512
KP = K // N
OG = F // N
HALVES = M // N
TILES = M // P


def tile_shifted_anomaly_product_h2_kernel(
    tc, x_words, x_scales, h_words, h_scales, r_inv, d, shift, out_0, out_1, out_2
):
    nc = tc.nc
    with ExitStack() as ctx:
        keep = ctx.enter_context(tc.tile_pool(name="keep", bufs=1))
        flow = ctx.enter_context(tc.tile_pool(name="flow", bufs=2))
        acc_pool = ctx.enter_context(tc.psum_pool(name="acc", bufs=5))
        turn_pool = ctx.enter_context(tc.psum_pool(name="turn", bufs=3))
        ctx.enter_context(tc.manual_schedule())

        def kept(shape, dtype, name):
            return keep.tile(shape, dtype, name=name, align_bytes=64)

        def load_scale_rows(plane, rows):
            for q in range(4):
                nc.sync.dma_start(
                    out=plane[32 * q : 32 * q + 4, :, :].bitcast(I32),
                    in_=rows[:, 4 * q : 4 * q + 4, :].rearrange("k r n -> r k n").bitcast(I32),
                )

        def zero_plane(plane):
            nc.vector.memset(plane[:].rearrange("p k n -> p (k n)").bitcast(I32), 0)

        def load_h(g, k0, nk):
            raw = kept([P, nk, 2 * N], U8, "h_raw_%d_%d" % (g, k0))
            nc.sync.dma_start(
                out=raw[:].bitcast(I32),
                in_=h_words[k0 : k0 + nk, :, 2 * N * g : 2 * N * (g + 1)].rearrange("k p n -> p k n").bitcast(I32),
            )
            return raw

        x_codes = {}

        def load_x(h, k0, nk):
            t_x = kept([P, nk, 4 * N], U8, "x_%d_%d" % (h, k0))
            nc.sync.dma_start(
                out=t_x[:].bitcast(I32),
                in_=x_words[k0 : k0 + nk].rearrange("k p n t -> p k (n t)")[:, :, 4 * N * h : 4 * N * (h + 1)].bitcast(I32),
            )
            for k in range(nk):
                x_codes[h, k0 + k] = t_x[:, k, :]

        d_raw = {}

        def load_d(pair):
            t_d = kept([P, 2, F], BF16, "d_raw_%d" % pair)
            nc.sync.dma_start(out=t_d[:], in_=d[2 * P * pair : 2 * P * (pair + 1), :].rearrange("(a p) o -> p a o", p=P))
            d_raw[pair] = t_d

        h_codes = {}
        h_planes = {}

        def sort_h_codes(g, k0, raw):
            nk = raw.shape[1]
            t_h = kept([P, nk, 4, 2 * P], U8, "h_%d_%d" % (g, k0))
            nc.vector.tensor_copy(
                out=t_h[:].bitcast(I32).rearrange("p k t (q w) -> p k t q w", w=4),
                in_=raw[:].bitcast(I32).rearrange("p k (q t w) -> p k t q w", t=4, w=4),
            )
            for k in range(nk):
                h_codes[g, k0 + k] = t_h[:, k, :, :]

        def sort_h_scales(g, raw):
            t_s = kept([P, KP, 4, P], U8, "h_plane_%d" % g)
            nc.vector.tensor_copy(
                out=t_s[:].bitcast(I32).rearrange("p k t (q w) -> p k t q w", w=2),
                in_=raw.bitcast(I32).rearrange("p k (q t w) -> p k t q w", t=4, w=2),
            )
            h_planes[g] = t_s

        r_raw = kept([P, N], BF16, "r_raw")
        nc.scalar.dma_start(out=r_raw[0:OG, :], in_=r_inv.rearrange("(g n) -> g n", g=OG))
        ident = kept([P, P], F32, "ident")
        make_identity(nc, ident[:])

        hs_raw_first = kept([P, KP, N], U8, "hs_raw_first")
        hs_raw_rest = kept([P, KP, 2 * N], U8, "hs_raw_rest")
        x_planes = [kept([P, KP, N], U8, "x_plane_%d" % h) for h in range(HALVES)]
        r_rows = kept([P, 4, P], F32, "r_rows")
        shift_rows = kept([P, P], F32, "shift_rows")
        zero_plane(hs_raw_first)
        zero_plane(x_planes[0])
        nc.vector.memset(r_rows[:], 0.0)
        zero_plane(hs_raw_rest)
        zero_plane(x_planes[1])
        nc.vector.memset(shift_rows[:], 0.0)

        h_raw_00 = load_h(0, 0, 2)
        load_x(0, 0, 1)
        load_scale_rows(hs_raw_first, h_scales[:, :, 0:N])
        load_scale_rows(x_planes[0], x_scales[:, :, 0:N])
        load_x(0, 1, 1)
        h_raw_02 = load_h(0, 2, 2)
        load_x(0, 2, 1)
        load_x(0, 3, 1)
        load_scale_rows(hs_raw_rest, h_scales[:, :, N:F])
        h_raw_1 = load_h(1, 0, KP)
        h_raw_2 = load_h(2, 0, KP)
        load_scale_rows(x_planes[1], x_scales[:, :, N:M])
        shift_raw = kept([P, P], BF16, "shift_raw")
        nc.sync.dma_start(out=shift_raw[0:TILES, :], in_=shift.rearrange("(c p) -> c p", p=P))
        load_d(0)
        load_x(1, 0, 2)
        load_x(1, 2, 2)
        for pair in range(1, 4):
            load_d(pair)

        nc.vector.tensor_copy(
            out=r_rows[0:OG, :, :].rearrange("g t (q r) -> g t q r", r=8),
            in_=r_raw[0:OG, :].rearrange("g (q t r) -> g t q r", t=4, r=8),
        )
        sort_h_codes(0, 0, h_raw_00)
        sort_h_scales(0, hs_raw_first[:])
        sort_h_codes(0, 2, h_raw_02)

        r_bank = turn_pool.tile([P, 4, P], F32, tag="turn", name="r_bank")
        for t in range(4):
            nc.tensor.transpose(r_bank[:, t, :], r_rows[:, t, :], ident[:])
        r_cols = kept([P, 4, OG], F32, "r_cols")
        nc.scalar.activation(out=r_cols[:], in_=r_bank[:, :, 0:OG], func=COPY)

        sort_h_scales(1, hs_raw_rest[:, :, 0:N])
        sort_h_codes(1, 0, h_raw_1)
        sort_h_scales(2, hs_raw_rest[:, :, N : 2 * N])
        sort_h_codes(2, 0, h_raw_2)
        nc.vector.tensor_copy(out=shift_rows[0:TILES, :], in_=shift_raw[0:TILES, :])
        shift_cols = kept([P, TILES], F32, "shift_cols")

        z_codes = [kept([P, OG, 4 * N], U8, "z_codes_%d" % h) for h in range(HALVES)]
        z_planes = [kept([P, OG, N], U8, "z_plane_%d" % h) for h in range(HALVES)]
        d_codes = kept([P, OG, 4 * M], U8, "d_codes")
        d_plane = kept([P, OG, M], U8, "d_plane")
        y_codes = kept([P, HALVES, 4 * M], U8, "y_codes")
        y_plane = kept([P, HALVES, M], U8, "y_plane")

        def first_pass(bank, h, g, t, k):
            nc.tensor.matmul_mx(
                out=bank[:],
                lhsT=h_codes[g, k][:, t, :].bitcast(FP4X4),
                lhsT_scale=h_planes[g][:, k, t, :],
                rhs=x_codes[h, k].bitcast(FP8X4),
                rhs_scale=x_planes[h][:, k, :],
                start=(k == 0),
                stop=(k == KP - 1),
            )

        def first_product(h, g, k_outer):
            z_flat = flow.tile([P, 4, N], BF16, tag="z_flat", name="z_flat", align_bytes=64)
            banks = []
            if k_outer:
                for t in range(4):
                    banks.append(acc_pool.tile([P, N], F32, tag="acc", name="acc"))
                for k in range(KP - 1):
                    for t in range(4):
                        first_pass(banks[t], h, g, t, k)
            for t in range(4):
                if not k_outer:
                    banks.append(acc_pool.tile([P, N], F32, tag="acc", name="acc"))
                for k in range(KP - 1 if k_outer else 0, KP):
                    first_pass(banks[t], h, g, t, k)
                nc.scalar.activation(out=z_flat[:, t, :], in_=banks[t][:], func=COPY, scale=r_cols[:, t, g : g + 1])
            return z_flat

        def interleave_z(z_flat):
            z_words = flow.tile([P, N, 4], BF16, tag="z_words", name="z_words", align_bytes=64)
            nc.vector.tensor_copy(
                out=z_words[:].rearrange("p (c i) t -> p c t i", i=4),
                in_=z_flat[:].rearrange("p t (c i) -> p c t i", i=4),
            )
            return z_words

        def quantize(words, codes, plane, g, col0):
            width = words.shape[1]
            nc.vector.quantize_mx(
                out=codes[:, g, 4 * col0 : 4 * (col0 + width)].bitcast(FP8X4),
                scales=plane[:, g, col0 : col0 + width],
                in_=words[:].rearrange("p n t -> p (n t)"),
            )

        def sort_d(pair, a):
            t_s = flow.tile([P, 2, F // 32, 8, 2], BF16, tag="d_sorted", name="d_sorted", bufs=4, align_bytes=64)
            nc.vector.tensor_copy(out=t_s[:], in_=d_raw[pair][:, a, :].rearrange("p (b u e r) -> p u b r e", u=2, e=2, r=8))
            return t_s[:].rearrange("p u b r e -> p (u b r e)").bitcast(F32)

        def turn(sources):
            bank = turn_pool.tile([P, 4, P], F32, tag="turn", name="turn")
            for n, source in enumerate(sources):
                nc.tensor.transpose(bank[:, n, :], source, ident[:])
            return bank

        def empty_turned(bank, count):
            words = flow.tile([P, count * P, 4], BF16, tag="turned", name="turned", bufs=6, align_bytes=64)
            nc.scalar.copy(
                out=words[:].bitcast(F32).rearrange("p (a n) u -> p a n u", a=count),
                in_=bank[:, 0 : 2 * count, :].rearrange("p (a u) n -> p a n u", u=2),
            )
            return words

        def turn_d(sorted_pair):
            half = F // 4
            banks = []
            for g in range(OG):
                banks.append(turn([s[:, u * half + g * P : u * half + (g + 1) * P] for s in sorted_pair for u in range(2)]))
            return [empty_turned(bank, 2) for bank in banks]

        groups = [(h, g) for h in range(HALVES) for g in range(OG)]
        z_flat, d_sorted, d_words = {}, {}, {}
        for s in range(len(groups) + 1):
            if s == 2:
                shift_bank = acc_pool.tile([P, N], F32, tag="acc", name="shift_bank")
                nc.tensor.transpose(shift_bank[:, 0:P], shift_rows[:], ident[:])
                nc.scalar.copy(out=shift_cols[:], in_=shift_bank[:, 0:TILES])
            if 0 <= s - 2 < 4:
                d_words[s - 2] = turn_d(d_sorted[s - 2])
            if s < len(groups):
                z_flat[s] = first_product(groups[s][0], groups[s][1], s == 0)
            if 0 <= s - 1 < 4:
                d_sorted[s - 1] = [sort_d(s - 1, a) for a in range(2)]
            if s >= 1:
                z_words = interleave_z(z_flat[s - 1])
            if 0 <= s - 2 < 4:
                for g in range(OG):
                    quantize(d_words[s - 2][g], d_codes, d_plane, g, 2 * P * (s - 2))
            if s >= 1:
                quantize(z_words, z_codes[groups[s - 1][0]], z_planes[groups[s - 1][0]], groups[s - 1][1], 0)

        y_pairs = {}

        def second_product(c):
            h, col = divmod(c * P, N)
            y_f32 = flow.tile([P, M], F32, tag="y_f32", name="y_f32", bufs=4, align_bytes=64)
            for jh in (h, 1 - h):
                bank = acc_pool.tile([P, N], F32, tag="acc", name="acc")
                for g in range(OG):
                    nc.tensor.matmul_mx(
                        out=bank[:],
                        lhsT=z_codes[h][:, g, 4 * col : 4 * (col + P)].bitcast(FP8X4),
                        lhsT_scale=z_planes[h][:, g, col : col + P],
                        rhs=d_codes[:, g, 4 * N * jh : 4 * N * (jh + 1)].bitcast(FP8X4),
                        rhs_scale=d_plane[:, g, N * jh : N * (jh + 1)],
                        start=(g == 0),
                        stop=(g == OG - 1),
                    )
                cols = slice(N * jh, N * (jh + 1))
                nc.scalar.copy(out=y_f32[:, cols], in_=bank[:])
                if jh == h:
                    diag = y_f32[:, c * P : (c + 1) * P]
                    nc.vector.scalar_tensor_tensor(
                        out=diag, in0=ident[:], scalar=shift_cols[:, c : c + 1], in1=diag,
                        op0=ALU.mult, op1=ALU.add,
                    )
                pairs = flow.tile([P, 2, P, 2], BF16, tag="y_pairs", name="y_pairs", bufs=8, align_bytes=64)
                nc.vector.tensor_copy(out=pairs[:], in_=y_f32[:, cols].rearrange("p (m u e) -> p u m e", u=2, e=2))
                y_pairs[c, jh] = pairs[:].rearrange("p u m e -> p (u m e)").bitcast(F32)
                if c == TILES - 1:
                    nc.sync.dma_start(out=out_0[c * P : (c + 1) * P, cols], in_=y_f32[:, cols])
            if c < TILES - 1:
                nc.sync.dma_start(out=out_0[c * P : (c + 1) * P, :], in_=y_f32[:])

        def turn_y(tiles, order):
            for g in order:
                bank = turn([y_pairs[c, g][:, u * P : (u + 1) * P] for c in tiles for u in range(2)])
                quantize(empty_turned(bank, len(tiles)), y_codes, y_plane, g, tiles[0] * P)

        def store_codes(col0, col1):
            nc.sync.dma_start(
                out=out_1.rearrange("g p n t -> p g (n t)")[:, :, 4 * col0 : 4 * col1].bitcast(I32),
                in_=y_codes[:, :, 4 * col0 : 4 * col1].bitcast(I32),
            )

        def store_scales(col0, col1):
            for q in range(4):
                nc.sync.dma_start(
                    out=out_2[:, 4 * q : 4 * q + 4, col0:col1].rearrange("g r n -> r g n").bitcast(I32),
                    in_=y_plane[32 * q : 32 * q + 4, :, col0:col1].bitcast(I32),
                )

        for c in range(4):
            second_product(c)
        turn_y([0, 1], (0, 1))
        store_codes(0, 2 * P)
        second_product(4)
        second_product(5)
        turn_y([2, 3], (0, 1))
        store_codes(2 * P, 4 * P)
        second_product(6)
        turn_y([4, 5], (0, 1))
        store_codes(4 * P, 6 * P)
        store_scales(0, 6 * P)
        second_product(7)
        turn_y([6], (1, 0))
        turn_y([7], (1, 0))
        store_codes(6 * P, M)
        store_scales(6 * P, M)
